import numpy as np
import ml_dtypes


def mxq(x, axis, fmt="e4m3"):
    dtype, down = {"e4m3": (ml_dtypes.float8_e4m3fn, 7), "e5m2": (ml_dtypes.float8_e5m2, 14)}[fmt]
    v = np.moveaxis(np.asarray(x, np.float32).astype(ml_dtypes.bfloat16).astype(np.float64), axis, -1)
    blocks = v.reshape(v.shape[:-1] + (-1, 32))
    amax = np.abs(blocks).max(-1, keepdims=True)
    byte = np.maximum(np.where(amax > 0, np.frexp(amax)[1] - 1 + 127, 0) - down, 1)
    scale = np.exp2(byte - 127.0)
    codes = (blocks / scale).astype(np.float32).astype(dtype).astype(np.float64)
    return np.moveaxis((codes * scale).reshape(v.shape), -1, axis)


WIDE = False


def mx_kscale(k):
    if not WIDE:
        return np.ones(k)
    levels = np.array([10, -10, 5, -5, 0])
    if k % 512:
        return np.exp2(np.random.permutation(np.resize(levels, k // 32))).repeat(32)
    a = np.empty((k // 512, 16))
    for p in range(k // 512):
        a[p, :8] = np.random.permutation(np.resize(levels, 8))
        for g in range(8):
            far = levels[np.abs(levels - a[p, g]) >= 10]
            a[p, g + 8] = far[np.random.randint(len(far))]
    return np.exp2(a.ravel()).repeat(32)


def f64(x):
    return np.asarray(x).astype(np.float64)


def striped(idx):
    return np.tile(idx.reshape(-1, 16).T, (8, 1)).astype(np.uint16)


def unstriped(offs):
    return offs[:16].T.reshape(-1).astype(np.int64)


def pack_weight(w):
    k, n = w.shape
    w = f64(np.asarray(w, np.float32).astype(ml_dtypes.bfloat16)).reshape(k // 32, 32, n)
    amax = np.abs(w).max(1)
    byte = np.clip(np.where(amax > 0, np.frexp(amax)[1] - 1 + 127 - 7, 1), 1, 254)
    scaled = (w * np.exp2(127.0 - byte)[:, None, :]).reshape(k, n).astype(np.float32)
    words = np.ascontiguousarray(scaled.reshape(k // 512, 128, 4, n).transpose(0, 1, 3, 2)).astype(ml_dtypes.float8_e4m3fn).view(np.uint8)
    return words, np.ascontiguousarray(byte.astype(np.uint8).reshape(k // 512, 16, n))


def unpack_weight(words, scales):
    g, p, n, _ = words.shape
    vals = np.ascontiguousarray(words).view(ml_dtypes.float8_e4m3fn).astype(np.float64) * np.repeat(np.exp2(scales.astype(np.float64) - 127.0), 8, axis=1)[..., None]
    return vals.transpose(0, 1, 3, 2).reshape(g * 512, n)


def sigmoid(v):
    return 1.0 / (1.0 + np.exp(-np.maximum(v, -700.0)))


H, K, T, S, D, N = 512, 1024, 4096, 1024, 4, 256
P = 2 ** 7


def setup_inputs():
    n = np.random.standard_normal
    s = mx_kscale(K)[:, None]
    u = mx_kscale(H)
    packed_xT = pack_weight(n((K, T)) * s)
    return {
        "x_words": packed_xT[0],
        "x_scales": packed_xT[1],
        "w1": (n((K, H)) / np.sqrt(K) / s).astype(np.float32),
        "logt": (np.tile(n(S), (P, 1))).astype(np.float32),
        "unit": (np.random.uniform(0.5, 1.5, (H, 1)) * u[:, None]).astype(np.float32),
        "wo": (n((H, N)) / np.sqrt(H) / u[:, None]).astype(np.float32),
        "offs": striped(np.random.permutation(T)[:S]),
    }


def reference(x_words, x_scales, w1, logt, unit, wo, offs):
    xq = unpack_weight(x_words, x_scales)[:, unstriped(offs)]
    y = mxq(f64(w1), 0, "e4m3").T @ xq
    px = sigmoid(y)
    hat = px * (-1.0 * px + 1.0) + 0.02
    lr = y - f64(logt)[:1]
    wl = hat * lr
    den = hat.reshape(len(hat), -1, D).sum(axis=2)
    rad = (wl.reshape(len(wl), -1, D).sum(axis=2)) / den
    zz = f64(unit) * rad
    return mxq(f64(wo), 0, "e4m3").T @ mxq(zz, 0, "e4m3")

@@ -1,0 +1,244 @@
+from contextlib import ExitStack
+
+import concourse.mybir as mybir
+from concourse.masks import make_identity
+
+K, H, T, S, D, N = 1024, 512, 4096, 1024, 4, 256
+V = S // D
+FLOPS = 2 * K * H * S + 2 * H * N * V
+BYTES = K * T + K * T // 32 + 4 * (K * H + S + H + H * N + N * V) + 2 * 128 * S // 16
+
+F32 = mybir.dt.float32
+BF16 = mybir.dt.bfloat16
+I32 = mybir.dt.int32
+U32 = mybir.dt.uint32
+U16 = mybir.dt.uint16
+U8 = mybir.dt.uint8
+FP8X4 = mybir.dt.float8_e4m3fn_x4
+ALU = mybir.AluOpType
+ACT = mybir.ActivationFunctionType
+
+P = 128
+PACK = 4
+PASSES = K // (P * PACK)
+BLOCKS = V // P
+HALF = P // 2
+
+
+def tile_picked_yhdrmg_mean_p_kernel(tc, x_words, x_scales, w1, logt, unit, wo, offs, out):
+    nc = tc.nc
+    with ExitStack() as ctx:
+        keep = ctx.enter_context(tc.tile_pool(name="keep", bufs=1))
+        stage = ctx.enter_context(tc.tile_pool(name="stage", bufs=1))
+        ring = ctx.enter_context(tc.tile_pool(name="ring", bufs=4))
+        ybanks = ctx.enter_context(tc.psum_pool(name="ybanks", bufs=4))
+        sums = ctx.enter_context(tc.psum_pool(name="sums", bufs=1))
+
+        offsets = keep.tile([P, S // 16], U16, name="offsets")
+        nc.sync.dma_start(offsets[:], offs)
+
+        scale_window = keep.tile([P, T], U8, name="scale_window", tag="early", align_bytes=64)
+        nc.vector.memset(scale_window[:].bitcast(I32), 0)
+        for q in range(4):
+            nc.gpsimd.dma_start(out=scale_window[32 * q : 32 * q + 8, :].bitcast(I32), in_=x_scales[:, 4 * q : 4 * q + 4, :].bitcast(I32))
+
+        word_window = []
+        for o in range(PASSES):
+            w = keep.tile([P, T], U32, name="word_window%d" % o)
+            nc.sync.dma_start(out=w[:].bitcast(I32), in_=x_words[o].rearrange("p n t -> p (n t)").bitcast(I32))
+            word_window.append(w)
+            if o == 0:
+                w1_raw0 = keep.tile([P, PACK, H], F32, name="w1_raw0")
+                nc.sync.dma_start(out=w1_raw0[:], in_=w1[0:512, :].rearrange("(p j) c -> p j c", j=PACK))
+
+        w1_raw1 = []
+        for h in range(2):
+            w = keep.tile([P, PACK, H // 2], F32, name="w1_raw1_%d" % h)
+            nc.sync.dma_start(out=w[:], in_=w1[512:1024, 256 * h : 256 * h + 256].rearrange("(p j) c -> p j c", j=PACK))
+            w1_raw1.append(w)
+
+        wo_raw = keep.tile([P, PACK, N], F32, name="wo_raw")
+        nc.sync.dma_start(out=wo_raw[:], in_=wo.rearrange("(p j) c -> p j c", j=PACK))
+        logt_sb = keep.tile([P, BLOCKS, D], F32, name="logt_sb")
+        nc.sync.dma_start(out=logt_sb[:], in_=logt[0].rearrange("(b p d) -> p b d", b=BLOCKS, d=D))
+        unit_sb = keep.tile([P, PACK], F32, name="unit_sb")
+        nc.sync.dma_start(out=unit_sb[:], in_=unit.rearrange("(p t) o -> p (t o)", t=PACK))
+
+        ident = keep.tile([P, P], F32, name="ident")
+        make_identity(nc, ident[:])
+
+        picked_scales = stage.tile([P, S], U8, name="picked_scales", tag="picked")
+        nc.vector.tensor_copy(picked_scales[:], scale_window[:].indirect(offsets[:]))
+        x_scale = []
+        for b in range(BLOCKS):
+            t = keep.tile([P, D, P], U8, name="x_scale%d" % b, align_bytes=64)
+            nc.vector.tensor_copy(
+                out=t[:].rearrange("p d (c i) -> p c d i", i=16),
+                in_=picked_scales[:, 512 * b : 512 * b + 512].rearrange("p (c i d) -> p c d i", i=16, d=D),
+            )
+            x_scale.append(t)
+
+        w1_bf = [
+            keep.tile([P, PACK, P, PACK], BF16, name="w1_bf0", tag="early", align_bytes=64),
+            keep.tile([P, PACK, P, PACK], BF16, name="w1_bf1", align_bytes=64),
+        ]
+        w1_codes = [keep.tile([P, H], U32, name="w1_codes%d" % o, align_bytes=64) for o in range(PASSES)]
+        w1_scale = [keep.tile([P, H], U8, name="w1_scale%d" % o, align_bytes=64) for o in range(PASSES)]
+        nc.scalar.copy(out=w1_bf[0][:].rearrange("p t m j -> p m t j"), in_=w1_raw0[:].rearrange("p j (m t) -> p m t j", t=PACK))
+        nc.vector.quantize_mx(out=w1_codes[0][:].bitcast(FP8X4), scales=w1_scale[0][:], in_=w1_bf[0][:].rearrange("p t m j -> p (t m j)"))
+
+        x_codes = {}
+
+        def pick_words(o, b):
+            picked = stage.tile([P, P * D], U32, name="picked_words%d_%d" % (o, b), tag="picked")
+            nc.vector.tensor_copy(picked[:], word_window[o][:].indirect(offsets[:, 32 * b : 32 * b + 32]))
+            dealt = keep.tile([P, D, P], U32, name="x_codes%d_%d" % (o, b), align_bytes=64)
+            nc.vector.tensor_copy(
+                out=dealt[:].rearrange("p d (c i) -> p c d i", i=4),
+                in_=picked[:].rearrange("p (c i d) -> p c d i", i=4, d=D),
+            )
+            x_codes[o, b] = dealt
+
+        pick_words(0, 0)
+        pick_words(0, 1)
+        pick_words(1, 0)
+
+        for h in range(2):
+            ms = slice(HALF * h, HALF * h + HALF)
+            dst = w1_bf[1][:, :, ms, :].rearrange("p t m j -> p m t j")
+            src = w1_raw1[h][:].rearrange("p j (m t) -> p m t j", t=PACK)
+            if h == 0:
+                nc.scalar.copy(out=dst, in_=src)
+            else:
+                nc.vector.tensor_copy(out=dst[:, 0:40], in_=src[:, 0:40])
+                nc.scalar.copy(out=dst[:, 40:HALF], in_=src[:, 40:HALF])
+            for t in range(PACK):
+                cols = slice(P * t + HALF * h, P * t + HALF * h + HALF)
+                nc.vector.quantize_mx(
+                    out=w1_codes[1][:, cols].bitcast(FP8X4),
+                    scales=w1_scale[1][:, cols],
+                    in_=w1_bf[1][:, t, ms, :].rearrange("p m j -> p (m j)"),
+                )
+
+        pick_words(1, 1)
+
+        wo_bf = keep.tile([P, N, PACK], BF16, name="wo_bf", align_bytes=64)
+        nc.gpsimd.tensor_scalar(
+            out=wo_bf[:].rearrange("p (c i) t -> p c t i", i=4),
+            in0=wo_raw[:].rearrange("p t (c i) -> p c t i", i=4),
+            scalar1=1.0,
+            scalar2=0.0,
+            op0=ALU.mult,
+            op1=ALU.add,
+        )
+        wo_codes = keep.tile([P, N], U32, name="wo_codes", align_bytes=64)
+        wo_scale = keep.tile([P, N], U8, name="wo_scale", align_bytes=64)
+        nc.vector.quantize_mx(out=wo_codes[:].bitcast(FP8X4), scales=wo_scale[:], in_=wo_bf[:].rearrange("p c t -> p (c t)"))
+
+        den = [sums.tile([P, PACK, P], F32, name="den%d" % b) for b in range(BLOCKS)]
+        num = [sums.tile([P, PACK, P], F32, name="num%d" % b) for b in range(BLOCKS)]
+
+        tiles = [(b, d) for b in range(BLOCKS) for d in range(D)]
+        ys, ths, hats = {}, {}, {}
+
+        def product(u):
+            b, d = tiles[u]
+            y = ybanks.tile([P, H], F32, name="y")
+            for o in range(PASSES):
+                nc.tensor.matmul_mx(
+                    out=y[:],
+                    lhsT=x_codes[o, b][:, d, :].bitcast(FP8X4),
+                    lhsT_scale=x_scale[b][4 * o :, d, :],
+                    rhs=w1_codes[o][:].bitcast(FP8X4),
+                    rhs_scale=w1_scale[o][:],
+                    start=(o == 0),
+                    stop=(o == PASSES - 1),
+                )
+            if u == len(tiles) - 1:
+                th = keep.tile([P, H], F32, name="th_last", tag="last")
+            else:
+                th = ring.tile([P, H], F32, name="th")
+            nc.scalar.activation(out=th[:], in_=y[:], func=ACT.Tanh, scale=0.5)
+            ys[u], ths[u] = y, th
+
+        def weight(u):
+            th = ths[u]
+            sq = ring.tile([P, H], F32, name="sq")
+            if u in (1, 3, 5, 7):
+                nc.vector.tensor_tensor(out=sq[:], in0=th[:], in1=th[:], op=ALU.mult)
+            else:
+                nc.scalar.activation(out=sq[:], in_=th[:], func=ACT.Square)
+            hat = ring.tile([P, H], F32, name="hat")
+            eng = nc.gpsimd if u in range(8) else nc.vector
+            eng.tensor_scalar(out=hat[:], in0=sq[:], scalar1=-0.25, scalar2=0.27, op0=ALU.mult, op1=ALU.add)
+            hats[u] = hat
+
+        def add_turned(u, src, acc):
+            d = tiles[u][1]
+            for t in range(PACK):
+                nc.tensor.matmul(
+                    out=acc[:, t, :],
+                    lhsT=src[:, P * t : P * t + P],
+                    rhs=ident[:],
+                    is_transpose=True,
+                    start=(d == 0 and t == 0),
+                    stop=(d == D - 1 and t == PACK - 1),
+                )
+
+        def weighted(u):
+            b, d = tiles[u]
+            wl = ring.tile([P, H], F32, name="wl")
+            nc.vector.scalar_tensor_tensor(
+                out=wl[:], in0=ys[u][:], scalar=logt_sb[:, b, d : d + 1], in1=hats[u][:], op0=ALU.subtract, op1=ALU.mult
+            )
+            add_turned(u, hats[u], den[b])
+            add_turned(u, wl, num[b])
+
+        for step in range(len(tiles) + 2):
+            if step < len(tiles):
+                product(step)
+            if 1 <= step <= len(tiles):
+                weight(step - 1)
+            if step >= 2:
+                weighted(step - 2)
+
+        for b in range(BLOCKS):
+            if b == 0:
+                rs = keep.tile([P, H], F32, name="rs0", tag="last")
+            else:
+                rs = keep.tile([P, H], F32, name="rs1")
+            nc.scalar.activation(out=rs[:], in_=den[b][:].rearrange("p t v -> p (t v)"), func=ACT.Abs_reciprocal_sqrt)
+            part = keep.tile([P, H], F32, name="part%d" % b)
+            for t in range(PACK):
+                cols = slice(P * t, P * t + P)
+                nc.vector.scalar_tensor_tensor(
+                    out=part[:, cols], in0=num[b][:, t, :], scalar=unit_sb[:, t : t + 1], in1=rs[:, cols], op0=ALU.mult, op1=ALU.mult
+                )
+            zz = keep.tile([P, P, PACK], BF16, name="zz%d" % b, align_bytes=64)
+            nc.vector.tensor_tensor(
+                out=zz[:].rearrange("p (c i) t -> p c t i", i=4),
+                in0=part[:].rearrange("p (t c i) -> p c t i", t=PACK, i=4),
+                in1=rs[:].rearrange("p (t c i) -> p c t i", t=PACK, i=4),
+                op=ALU.mult,
+            )
+            zz_codes = keep.tile([P, P], U32, name="zz_codes%d" % b, align_bytes=64)
+            zz_scale = keep.tile([P, P], U8, name="zz_scale%d" % b, align_bytes=64)
+            nc.vector.quantize_mx(out=zz_codes[:].bitcast(FP8X4), scales=zz_scale[:], in_=zz[:].rearrange("p v t -> p (v t)"))
+            acc = ybanks.tile([P, H], F32, name="y")
+            for m in range(N // P):
+                cols = slice(P * m, P * m + P)
+                nc.tensor.matmul_mx(
+                    out=acc[:, cols],
+                    lhsT=wo_codes[:, cols].bitcast(FP8X4),
+                    lhsT_scale=wo_scale[:, cols],
+                    rhs=zz_codes[:].bitcast(FP8X4),
+                    rhs_scale=zz_scale[:],
+                    start=True,
+                    stop=True,
+                )
+            res = keep.tile([P, N], F32, name="res%d" % b)
+            nc.scalar.copy(out=res[:], in_=acc[:, 0:N])
+            nc.sync.dma_start(
+                out=out[:, P * b : P * b + P].rearrange("(m p) v -> p m v", p=P),
+                in_=res[:].rearrange("p (m v) -> p m v", v=P),
+            )

@@ -29,9 +29,8 @@ def tile_picked_yhdrmg_mean_p_kernel(tc, x_words, x_scales, w1, logt, unit, wo, 
     nc = tc.nc
     with ExitStack() as ctx:
         keep = ctx.enter_context(tc.tile_pool(name="keep", bufs=1))
-        stage = ctx.enter_context(tc.tile_pool(name="stage", bufs=1))
-        ring = ctx.enter_context(tc.tile_pool(name="ring", bufs=4))
-        ybanks = ctx.enter_context(tc.psum_pool(name="ybanks", bufs=4))
+        ring = ctx.enter_context(tc.tile_pool(name="ring", bufs=8))
+        ybanks = ctx.enter_context(tc.psum_pool(name="ybanks", bufs=6))
         sums = ctx.enter_context(tc.psum_pool(name="sums", bufs=1))
 
         offsets = keep.tile([P, S // 16], U16, name="offsets")
@@ -39,21 +38,24 @@ def tile_picked_yhdrmg_mean_p_kernel(tc, x_words, x_scales, w1, logt, unit, wo, 
 
         scale_window = keep.tile([P, T], U8, name="scale_window", tag="early", align_bytes=64)
         nc.vector.memset(scale_window[:].bitcast(I32), 0)
-        for q in range(4):
-            nc.gpsimd.dma_start(out=scale_window[32 * q : 32 * q + 8, :].bitcast(I32), in_=x_scales[:, 4 * q : 4 * q + 4, :].bitcast(I32))
+        word_window = [keep.tile([P, T], U32, name="word_window%d" % o) for o in range(PASSES)]
 
-        word_window = []
+        def load_words(o, cols):
+            src = x_words[o, :, cols, :].rearrange("p n t -> p (n t)").bitcast(I32)
+            nc.sync.dma_start(out=word_window[o][:, cols].bitcast(I32), in_=src)
+
         for o in range(PASSES):
-            w = keep.tile([P, T], U32, name="word_window%d" % o)
-            nc.sync.dma_start(out=w[:].bitcast(I32), in_=x_words[o].rearrange("p n t -> p (n t)").bitcast(I32))
-            word_window.append(w)
-            if o == 0:
-                w1_raw0 = keep.tile([P, PACK, H], F32, name="w1_raw0")
-                nc.sync.dma_start(out=w1_raw0[:], in_=w1[0:512, :].rearrange("(p j) c -> p j c", j=PACK))
+            load_words(0, slice(o * T // 2, (o + 1) * T // 2))
+            for q in range(4):
+                r = 32 * q + 4 * o
+                nc.sync.dma_start(out=scale_window[r : r + 4, :].bitcast(I32), in_=x_scales[o, 4 * q : 4 * q + 4, :].bitcast(I32))
+        w1_raw0 = keep.tile([P, PACK, H], F32, name="w1_raw0")
+        nc.sync.dma_start(out=w1_raw0[:], in_=w1[0:512, :].rearrange("(p j) c -> p j c", j=PACK))
+        load_words(1, slice(0, T))
 
         w1_raw1 = []
         for h in range(2):
-            w = keep.tile([P, PACK, H // 2], F32, name="w1_raw1_%d" % h)
+            w = keep.tile([P, PACK, H // 2], F32, name="w1_raw1_%d" % h, tag="raw1_%d" % h, align_bytes=64)
             nc.sync.dma_start(out=w[:], in_=w1[512:1024, 256 * h : 256 * h + 256].rearrange("(p j) c -> p j c", j=PACK))
             w1_raw1.append(w)
 
@@ -67,30 +69,40 @@ def tile_picked_yhdrmg_mean_p_kernel(tc, x_words, x_scales, w1, logt, unit, wo, 
         ident = keep.tile([P, P], F32, name="ident")
         make_identity(nc, ident[:])
 
-        picked_scales = stage.tile([P, S], U8, name="picked_scales", tag="picked")
+        picked_scales = keep.tile([P, S], U8, name="picked_scales")
         nc.vector.tensor_copy(picked_scales[:], scale_window[:].indirect(offsets[:]))
-        x_scale = []
-        for b in range(BLOCKS):
-            t = keep.tile([P, D, P], U8, name="x_scale%d" % b, align_bytes=64)
-            nc.vector.tensor_copy(
-                out=t[:].rearrange("p d (c i) -> p c d i", i=16),
-                in_=picked_scales[:, 512 * b : 512 * b + 512].rearrange("p (c i d) -> p c d i", i=16, d=D),
-            )
-            x_scale.append(t)
+        x_scale = keep.tile([P, D, V], U8, name="x_scale", align_bytes=64)
+        picked_first = keep.tile([P, S], U32, name="picked_first")
+        nc.vector.tensor_copy(picked_first[:], word_window[0][:].indirect(offsets[:]))
+        nc.vector.tensor_copy(
+            out=x_scale[:].rearrange("p d (c i) -> p c d i", i=16),
+            in_=picked_scales[:].rearrange("p (c i d) -> p c d i", i=16, d=D),
+        )
+        codes_first = keep.tile([P, D, V], U32, name="codes_first", align_bytes=64)
+        nc.vector.tensor_copy(
+            out=codes_first[:].rearrange("p d (c i) -> p c d i", i=4),
+            in_=picked_first[:].rearrange("p (c i d) -> p c d i", i=4, d=D),
+        )
 
         w1_bf = [
-            keep.tile([P, PACK, P, PACK], BF16, name="w1_bf0", tag="early", align_bytes=64),
-            keep.tile([P, PACK, P, PACK], BF16, name="w1_bf1", align_bytes=64),
+            keep.tile([P, PACK, P, PACK], BF16, name="w1_bf0", tag="middle", align_bytes=64),
+            keep.tile([P, PACK, P, PACK], BF16, name="w1_bf1", tag="late", align_bytes=64),
         ]
-        w1_codes = [keep.tile([P, H], U32, name="w1_codes%d" % o, align_bytes=64) for o in range(PASSES)]
+        w1_codes = [
+            keep.tile([P, H], U32, name="w1_codes0", tag="early", align_bytes=64),
+            keep.tile([P, H], U32, name="w1_codes1", align_bytes=64),
+        ]
         w1_scale = [keep.tile([P, H], U8, name="w1_scale%d" % o, align_bytes=64) for o in range(PASSES)]
         nc.scalar.copy(out=w1_bf[0][:].rearrange("p t m j -> p m t j"), in_=w1_raw0[:].rearrange("p j (m t) -> p m t j", t=PACK))
         nc.vector.quantize_mx(out=w1_codes[0][:].bitcast(FP8X4), scales=w1_scale[0][:], in_=w1_bf[0][:].rearrange("p t m j -> p (t m j)"))
 
-        x_codes = {}
+        x_codes = {(0, b): codes_first[:, :, P * b : P * b + P] for b in range(BLOCKS)}
 
         def pick_words(o, b):
-            picked = stage.tile([P, P * D], U32, name="picked_words%d_%d" % (o, b), tag="picked")
+            if (o, b) == (1, 1):
+                picked = keep.tile([P, P * D], U32, name="picked_last", tag="late", align_bytes=64)
+            else:
+                picked = keep.tile([P, P * D], U32, name="picked_third", tag="middle", align_bytes=64)
             nc.vector.tensor_copy(picked[:], word_window[o][:].indirect(offsets[:, 32 * b : 32 * b + 32]))
             dealt = keep.tile([P, D, P], U32, name="x_codes%d_%d" % (o, b), align_bytes=64)
             nc.vector.tensor_copy(
@@ -99,8 +111,6 @@ def tile_picked_yhdrmg_mean_p_kernel(tc, x_words, x_scales, w1, logt, unit, wo, 
             )
             x_codes[o, b] = dealt
 
-        pick_words(0, 0)
-        pick_words(0, 1)
         pick_words(1, 0)
 
         for h in range(2):
@@ -110,66 +120,60 @@ def tile_picked_yhdrmg_mean_p_kernel(tc, x_words, x_scales, w1, logt, unit, wo, 
             if h == 0:
                 nc.scalar.copy(out=dst, in_=src)
             else:
-                nc.vector.tensor_copy(out=dst[:, 0:40], in_=src[:, 0:40])
-                nc.scalar.copy(out=dst[:, 40:HALF], in_=src[:, 40:HALF])
-            for t in range(PACK):
-                cols = slice(P * t + HALF * h, P * t + HALF * h + HALF)
-                nc.vector.quantize_mx(
-                    out=w1_codes[1][:, cols].bitcast(FP8X4),
-                    scales=w1_scale[1][:, cols],
-                    in_=w1_bf[1][:, t, ms, :].rearrange("p m j -> p (m j)"),
-                )
+                nc.vector.tensor_copy(out=dst[:, 0:48], in_=src[:, 0:48])
+                nc.scalar.copy(out=dst[:, 48:HALF], in_=src[:, 48:HALF])
+        nc.vector.quantize_mx(out=w1_codes[1][:].bitcast(FP8X4), scales=w1_scale[1][:], in_=w1_bf[1][:].rearrange("p t m j -> p (t m j)"))
 
         pick_words(1, 1)
 
-        wo_bf = keep.tile([P, N, PACK], BF16, name="wo_bf", align_bytes=64)
-        nc.gpsimd.tensor_scalar(
-            out=wo_bf[:].rearrange("p (c i) t -> p c t i", i=4),
-            in0=wo_raw[:].rearrange("p t (c i) -> p c t i", i=4),
-            scalar1=1.0,
-            scalar2=0.0,
-            op0=ALU.mult,
-            op1=ALU.add,
-        )
+        wo_bf = keep.tile([P, N, PACK], BF16, name="wo_bf", tag="raw1_1", align_bytes=64)
+        wo_dst = wo_bf[:].rearrange("p (c i) t -> p c t i", i=4)
+        wo_src = wo_raw[:].rearrange("p t (c i) -> p c t i", i=4)
+        nc.scalar.copy(out=wo_dst[:, 0:32], in_=wo_src[:, 0:32])
+        nc.vector.tensor_copy(out=wo_dst[:, 32:64], in_=wo_src[:, 32:64])
         wo_codes = keep.tile([P, N], U32, name="wo_codes", align_bytes=64)
         wo_scale = keep.tile([P, N], U8, name="wo_scale", align_bytes=64)
         nc.vector.quantize_mx(out=wo_codes[:].bitcast(FP8X4), scales=wo_scale[:], in_=wo_bf[:].rearrange("p c t -> p (c t)"))
 
-        den = [sums.tile([P, PACK, P], F32, name="den%d" % b) for b in range(BLOCKS)]
-        num = [sums.tile([P, PACK, P], F32, name="num%d" % b) for b in range(BLOCKS)]
+        den = {0: sums.tile([P, PACK, P], F32, name="den0", tag="den")}
+        num = {0: sums.tile([P, PACK, P], F32, name="num0", tag="num")}
 
         tiles = [(b, d) for b in range(BLOCKS) for d in range(D)]
         ys, ths, hats = {}, {}, {}
 
         def product(u):
             b, d = tiles[u]
-            y = ybanks.tile([P, H], F32, name="y")
+            y = ybanks.tile([P, H], F32, name="y", tag="y")
             for o in range(PASSES):
                 nc.tensor.matmul_mx(
                     out=y[:],
                     lhsT=x_codes[o, b][:, d, :].bitcast(FP8X4),
-                    lhsT_scale=x_scale[b][4 * o :, d, :],
+                    lhsT_scale=x_scale[4 * o :, d, P * b : P * b + P],
                     rhs=w1_codes[o][:].bitcast(FP8X4),
                     rhs_scale=w1_scale[o][:],
                     start=(o == 0),
                     stop=(o == PASSES - 1),
                 )
+            ys[u] = y
+
+        def squash(u):
+            y = ys[u]
             if u == len(tiles) - 1:
                 th = keep.tile([P, H], F32, name="th_last", tag="last")
             else:
                 th = ring.tile([P, H], F32, name="th")
             nc.scalar.activation(out=th[:], in_=y[:], func=ACT.Tanh, scale=0.5)
-            ys[u], ths[u] = y, th
+            ths[u] = th
 
         def weight(u):
             th = ths[u]
             sq = ring.tile([P, H], F32, name="sq")
-            if u in (1, 3, 5, 7):
+            if u in (4,):
                 nc.vector.tensor_tensor(out=sq[:], in0=th[:], in1=th[:], op=ALU.mult)
             else:
                 nc.scalar.activation(out=sq[:], in_=th[:], func=ACT.Square)
             hat = ring.tile([P, H], F32, name="hat")
-            eng = nc.gpsimd if u in range(8) else nc.vector
+            eng = nc.gpsimd if u in () else nc.vector
             eng.tensor_scalar(out=hat[:], in0=sq[:], scalar1=-0.25, scalar2=0.27, op0=ALU.mult, op1=ALU.add)
             hats[u] = hat
 
@@ -191,12 +195,19 @@ def tile_picked_yhdrmg_mean_p_kernel(tc, x_words, x_scales, w1, logt, unit, wo, 
             nc.vector.scalar_tensor_tensor(
                 out=wl[:], in0=ys[u][:], scalar=logt_sb[:, b, d : d + 1], in1=hats[u][:], op0=ALU.subtract, op1=ALU.mult
             )
+            if (b, d) == (1, 0):
+                den[1] = ybanks.tile([P, PACK, P], F32, name="den1", tag="y")
+                num[1] = ybanks.tile([P, PACK, P], F32, name="num1", tag="y")
             add_turned(u, hats[u], den[b])
             add_turned(u, wl, num[b])
 
+        product(0)
+        product(1)
         for step in range(len(tiles) + 2):
+            if step + 2 < len(tiles):
+                product(step + 2)
             if step < len(tiles):
-                product(step)
+                squash(step)
             if 1 <= step <= len(tiles):
                 weight(step - 1)
             if step >= 2:
@@ -209,22 +220,30 @@ def tile_picked_yhdrmg_mean_p_kernel(tc, x_words, x_scales, w1, logt, unit, wo, 
                 rs = keep.tile([P, H], F32, name="rs1")
             nc.scalar.activation(out=rs[:], in_=den[b][:].rearrange("p t v -> p (t v)"), func=ACT.Abs_reciprocal_sqrt)
             part = keep.tile([P, H], F32, name="part%d" % b)
-            for t in range(PACK):
-                cols = slice(P * t, P * t + P)
-                nc.vector.scalar_tensor_tensor(
-                    out=part[:, cols], in0=num[b][:, t, :], scalar=unit_sb[:, t : t + 1], in1=rs[:, cols], op0=ALU.mult, op1=ALU.mult
-                )
+            if b == 0:
+                other = rs
+                for t in range(PACK):
+                    cols = slice(P * t, P * t + P)
+                    nc.vector.scalar_tensor_tensor(
+                        out=part[:, cols], in0=num[b][:, t, :], scalar=unit_sb[:, t : t + 1], in1=rs[:, cols], op0=ALU.mult, op1=ALU.mult
+                    )
+            else:
+                other = keep.tile([P, H], F32, name="inverse")
+                nc.scalar.activation(out=other[:], in_=rs[:], func=ACT.Square)
+                for t in range(PACK):
+                    cols = slice(P * t, P * t + P)
+                    nc.scalar.activation(out=part[:, cols], in_=num[b][:, t, :], func=ACT.Copy, scale=unit_sb[:, t : t + 1])
             zz = keep.tile([P, P, PACK], BF16, name="zz%d" % b, align_bytes=64)
             nc.vector.tensor_tensor(
                 out=zz[:].rearrange("p (c i) t -> p c t i", i=4),
                 in0=part[:].rearrange("p (t c i) -> p c t i", t=PACK, i=4),
-                in1=rs[:].rearrange("p (t c i) -> p c t i", t=PACK, i=4),
+                in1=other[:].rearrange("p (t c i) -> p c t i", t=PACK, i=4),
                 op=ALU.mult,
             )
             zz_codes = keep.tile([P, P], U32, name="zz_codes%d" % b, align_bytes=64)
             zz_scale = keep.tile([P, P], U8, name="zz_scale%d" % b, align_bytes=64)
             nc.vector.quantize_mx(out=zz_codes[:].bitcast(FP8X4), scales=zz_scale[:], in_=zz[:].rearrange("p v t -> p (v t)"))
-            acc = ybanks.tile([P, H], F32, name="y")
+            acc = ybanks.tile([P, H], F32, name="acc", tag="y")
             for m in range(N // P):
                 cols = slice(P * m, P * m + P)
                 nc.tensor.matmul_mx(

@@ -30,7 +30,7 @@ def tile_picked_yhdrmg_mean_p_kernel(tc, x_words, x_scales, w1, logt, unit, wo, 
     with ExitStack() as ctx:
         keep = ctx.enter_context(tc.tile_pool(name="keep", bufs=1))
         ring = ctx.enter_context(tc.tile_pool(name="ring", bufs=8))
-        ybanks = ctx.enter_context(tc.psum_pool(name="ybanks", bufs=6))
+        ybanks = ctx.enter_context(tc.psum_pool(name="ybanks", bufs=5))
         sums = ctx.enter_context(tc.psum_pool(name="sums", bufs=1))
 
         offsets = keep.tile([P, S // 16], U16, name="offsets")
@@ -69,19 +69,20 @@ def tile_picked_yhdrmg_mean_p_kernel(tc, x_words, x_scales, w1, logt, unit, wo, 
         ident = keep.tile([P, P], F32, name="ident")
         make_identity(nc, ident[:])
 
-        picked_scales = keep.tile([P, S], U8, name="picked_scales")
-        nc.vector.tensor_copy(picked_scales[:], scale_window[:].indirect(offsets[:]))
         x_scale = keep.tile([P, D, V], U8, name="x_scale", align_bytes=64)
-        picked_first = keep.tile([P, S], U32, name="picked_first")
+        picked_first = keep.tile([P, S], U32, name="picked_first", tag="first")
         nc.vector.tensor_copy(picked_first[:], word_window[0][:].indirect(offsets[:]))
-        nc.vector.tensor_copy(
-            out=x_scale[:].rearrange("p d (c i) -> p c d i", i=16),
-            in_=picked_scales[:].rearrange("p (c i d) -> p c d i", i=16, d=D),
-        )
         codes_first = keep.tile([P, D, V], U32, name="codes_first", align_bytes=64)
         nc.vector.tensor_copy(
             out=codes_first[:].rearrange("p d (c i) -> p c d i", i=4),
             in_=picked_first[:].rearrange("p (c i d) -> p c d i", i=4, d=D),
+        )
+
+        picked_scales = keep.tile([P, S], U8, name="picked_scales", tag="first")
+        nc.vector.tensor_copy(picked_scales[:], scale_window[:].indirect(offsets[:]))
+        nc.vector.tensor_copy(
+            out=x_scale[:].rearrange("p d (c i) -> p c d i", i=16),
+            in_=picked_scales[:].rearrange("p (c i d) -> p c d i", i=16, d=D),
         )
 
         w1_bf = [
@@ -117,11 +118,9 @@ def tile_picked_yhdrmg_mean_p_kernel(tc, x_words, x_scales, w1, logt, unit, wo, 
             ms = slice(HALF * h, HALF * h + HALF)
             dst = w1_bf[1][:, :, ms, :].rearrange("p t m j -> p m t j")
             src = w1_raw1[h][:].rearrange("p j (m t) -> p m t j", t=PACK)
-            if h == 0:
-                nc.scalar.copy(out=dst, in_=src)
-            else:
-                nc.vector.tensor_copy(out=dst[:, 0:48], in_=src[:, 0:48])
-                nc.scalar.copy(out=dst[:, 48:HALF], in_=src[:, 48:HALF])
+            cut = 16 if h == 0 else 48
+            nc.vector.tensor_copy(out=dst[:, 0:cut], in_=src[:, 0:cut])
+            nc.scalar.copy(out=dst[:, cut:HALF], in_=src[:, cut:HALF])
         nc.vector.quantize_mx(out=w1_codes[1][:].bitcast(FP8X4), scales=w1_scale[1][:], in_=w1_bf[1][:].rearrange("p t m j -> p (t m j)"))
 
         pick_words(1, 1)
@@ -158,7 +157,7 @@ def tile_picked_yhdrmg_mean_p_kernel(tc, x_words, x_scales, w1, logt, unit, wo, 
 
         def squash(u):
             y = ys[u]
-            if u == len(tiles) - 1:
+            if u == 6:
                 th = keep.tile([P, H], F32, name="th_last", tag="last")
             else:
                 th = ring.tile([P, H], F32, name="th")
@@ -168,12 +167,12 @@ def tile_picked_yhdrmg_mean_p_kernel(tc, x_words, x_scales, w1, logt, unit, wo, 
         def weight(u):
             th = ths[u]
             sq = ring.tile([P, H], F32, name="sq")
-            if u in (4,):
+            if u in (3, 5, 7):
                 nc.vector.tensor_tensor(out=sq[:], in0=th[:], in1=th[:], op=ALU.mult)
             else:
                 nc.scalar.activation(out=sq[:], in_=th[:], func=ACT.Square)
             hat = ring.tile([P, H], F32, name="hat")
-            eng = nc.gpsimd if u in () else nc.vector
+            eng = nc.gpsimd if u in range(8) else nc.vector
             eng.tensor_scalar(out=hat[:], in0=sq[:], scalar1=-0.25, scalar2=0.27, op0=ALU.mult, op1=ALU.add)
             hats[u] = hat
 
@@ -196,7 +195,7 @@ def tile_picked_yhdrmg_mean_p_kernel(tc, x_words, x_scales, w1, logt, unit, wo, 
                 out=wl[:], in0=ys[u][:], scalar=logt_sb[:, b, d : d + 1], in1=hats[u][:], op0=ALU.subtract, op1=ALU.mult
             )
             if (b, d) == (1, 0):
-                den[1] = ybanks.tile([P, PACK, P], F32, name="den1", tag="y")
+                den[1] = sums.tile([P, PACK, P], F32, name="den1")
                 num[1] = ybanks.tile([P, PACK, P], F32, name="num1", tag="y")
             add_turned(u, hats[u], den[b])
             add_turned(u, wl, num[b])
@@ -213,32 +212,31 @@ def tile_picked_yhdrmg_mean_p_kernel(tc, x_words, x_scales, w1, logt, unit, wo, 
             if step >= 2:
                 weighted(step - 2)
 
+        inverses = []
         for b in range(BLOCKS):
             if b == 0:
                 rs = keep.tile([P, H], F32, name="rs0", tag="last")
             else:
                 rs = keep.tile([P, H], F32, name="rs1")
-            nc.scalar.activation(out=rs[:], in_=den[b][:].rearrange("p t v -> p (t v)"), func=ACT.Abs_reciprocal_sqrt)
-            part = keep.tile([P, H], F32, name="part%d" % b)
-            if b == 0:
-                other = rs
-                for t in range(PACK):
-                    cols = slice(P * t, P * t + P)
-                    nc.vector.scalar_tensor_tensor(
-                        out=part[:, cols], in0=num[b][:, t, :], scalar=unit_sb[:, t : t + 1], in1=rs[:, cols], op0=ALU.mult, op1=ALU.mult
-                    )
-            else:
-                other = keep.tile([P, H], F32, name="inverse")
-                nc.scalar.activation(out=other[:], in_=rs[:], func=ACT.Square)
-                for t in range(PACK):
-                    cols = slice(P * t, P * t + P)
-                    nc.scalar.activation(out=part[:, cols], in_=num[b][:, t, :], func=ACT.Copy, scale=unit_sb[:, t : t + 1])
+            nc.scalar.activation(
+                out=rs[:].rearrange("p (v t) -> p v t", t=PACK), in_=den[b][:].rearrange("p t v -> p v t"), func=ACT.Abs_reciprocal_sqrt
+            )
+            inverse = keep.tile([P, H], F32, name="inverse%d" % b)
+            nc.scalar.activation(out=inverse[:], in_=rs[:], func=ACT.Square)
+            inverses.append(inverse)
+
+        for b in range(BLOCKS):
+            inverse = inverses[b]
+            scaled = keep.tile([P, P, PACK], F32, name="scaled%d" % b)
+            nc.vector.tensor_tensor(
+                out=scaled[:],
+                in0=num[b][:].rearrange("p t v -> p v t"),
+                in1=unit_sb[:].unsqueeze(1).to_broadcast([P, P, PACK]),
+                op=ALU.mult,
+            )
             zz = keep.tile([P, P, PACK], BF16, name="zz%d" % b, align_bytes=64)
             nc.vector.tensor_tensor(
-                out=zz[:].rearrange("p (c i) t -> p c t i", i=4),
-                in0=part[:].rearrange("p (t c i) -> p c t i", t=PACK, i=4),
-                in1=other[:].rearrange("p (t c i) -> p c t i", t=PACK, i=4),
-                op=ALU.mult,
+                out=zz[:].rearrange("p v t -> p (v t)"), in0=scaled[:].rearrange("p v t -> p (v t)"), in1=inverse[:], op=ALU.mult
             )
             zz_codes = keep.tile([P, P], U32, name="zz_codes%d" % b, align_bytes=64)
             zz_scale = keep.tile([P, P], U8, name="zz_scale%d" % b, align_bytes=64)

@@ -20,23 +20,33 @@ ACT = mybir.ActivationFunctionType
 
 P = 128
 PACK = 4
-PASSES = K // (P * PACK)
+K_PASS = P * PACK
+PASSES = K // K_PASS
 BLOCKS = V // P
-HALF = P // 2
+TILES = [(b, d) for b in range(BLOCKS) for d in range(D)]
+QUADRANT = 32
+SCALE_ROWS = 4
+LIST_COLS = P * D // 16
+LINE_WORDS, LINE_BYTES = 4, 16
+M_HALF = P // 2
+
+Y_BANKS = 6
+VECTOR_M = (16, 48)
+VECTOR_SQUARES = (3, 5)
 
 
 def tile_picked_yhdrmg_mean_p_kernel(tc, x_words, x_scales, w1, logt, unit, wo, offs, out):
     nc = tc.nc
     with ExitStack() as ctx:
         keep = ctx.enter_context(tc.tile_pool(name="keep", bufs=1))
-        ring = ctx.enter_context(tc.tile_pool(name="ring", bufs=8))
-        ybanks = ctx.enter_context(tc.psum_pool(name="ybanks", bufs=5))
+        ring = ctx.enter_context(tc.tile_pool(name="ring", bufs=len(TILES)))
+        ybanks = ctx.enter_context(tc.psum_pool(name="ybanks", bufs=Y_BANKS))
         sums = ctx.enter_context(tc.psum_pool(name="sums", bufs=1))
 
         offsets = keep.tile([P, S // 16], U16, name="offsets")
         nc.sync.dma_start(offsets[:], offs)
 
-        scale_window = keep.tile([P, T], U8, name="scale_window", tag="early", align_bytes=64)
+        scale_window = keep.tile([P, T], U8, name="scale_window", tag="scale_window", align_bytes=64)
         nc.vector.memset(scale_window[:].bitcast(I32), 0)
         word_window = [keep.tile([P, T], U32, name="word_window%d" % o) for o in range(PASSES)]
 
@@ -46,18 +56,21 @@ def tile_picked_yhdrmg_mean_p_kernel(tc, x_words, x_scales, w1, logt, unit, wo, 
 
         for o in range(PASSES):
             load_words(0, slice(o * T // 2, (o + 1) * T // 2))
-            for q in range(4):
-                r = 32 * q + 4 * o
-                nc.sync.dma_start(out=scale_window[r : r + 4, :].bitcast(I32), in_=x_scales[o, 4 * q : 4 * q + 4, :].bitcast(I32))
+            for r in range(SCALE_ROWS):
+                nc.sync.dma_start(
+                    out=scale_window[SCALE_ROWS * o + r : P : QUADRANT, :].bitcast(I32),
+                    in_=x_scales[o, r : K_PASS // 32 : SCALE_ROWS, :].bitcast(I32),
+                )
         w1_raw0 = keep.tile([P, PACK, H], F32, name="w1_raw0")
-        nc.sync.dma_start(out=w1_raw0[:], in_=w1[0:512, :].rearrange("(p j) c -> p j c", j=PACK))
+        nc.sync.dma_start(out=w1_raw0[:], in_=w1[0:K_PASS, :].rearrange("(p j) c -> p j c", j=PACK))
         load_words(1, slice(0, T))
 
         w1_raw1 = []
         for h in range(2):
-            w = keep.tile([P, PACK, H // 2], F32, name="w1_raw1_%d" % h, tag="raw1_%d" % h, align_bytes=64)
-            nc.sync.dma_start(out=w[:], in_=w1[512:1024, 256 * h : 256 * h + 256].rearrange("(p j) c -> p j c", j=PACK))
-            w1_raw1.append(w)
+            raw = keep.tile([P, PACK, H // 2], F32, name="w1_raw1_%d" % h, tag="w1_raw1_%d" % h, align_bytes=64)
+            cols = slice(h * H // 2, (h + 1) * H // 2)
+            nc.sync.dma_start(out=raw[:], in_=w1[K_PASS:K, cols].rearrange("(p j) c -> p j c", j=PACK))
+            w1_raw1.append(raw)
 
         wo_raw = keep.tile([P, PACK, N], F32, name="wo_raw")
         nc.sync.dma_start(out=wo_raw[:], in_=wo.rearrange("(p j) c -> p j c", j=PACK))
@@ -69,85 +82,80 @@ def tile_picked_yhdrmg_mean_p_kernel(tc, x_words, x_scales, w1, logt, unit, wo, 
         ident = keep.tile([P, P], F32, name="ident")
         make_identity(nc, ident[:])
 
+        def deal(dealt, picked, run):
+            nc.vector.tensor_copy(
+                out=dealt[:].rearrange("p d (c i) -> p c d i", i=run),
+                in_=picked[:].rearrange("p (c i d) -> p c d i", i=run, d=D),
+            )
+
         x_scale = keep.tile([P, D, V], U8, name="x_scale", align_bytes=64)
-        picked_first = keep.tile([P, S], U32, name="picked_first", tag="first")
-        nc.vector.tensor_copy(picked_first[:], word_window[0][:].indirect(offsets[:]))
-        codes_first = keep.tile([P, D, V], U32, name="codes_first", align_bytes=64)
-        nc.vector.tensor_copy(
-            out=codes_first[:].rearrange("p d (c i) -> p c d i", i=4),
-            in_=picked_first[:].rearrange("p (c i d) -> p c d i", i=4, d=D),
-        )
+        picked_pass0 = keep.tile([P, S], U32, name="picked_pass0", tag="picked_pass0")
+        nc.vector.tensor_copy(picked_pass0[:], word_window[0][:].indirect(offsets[:]))
+        codes_pass0 = keep.tile([P, D, V], U32, name="codes_pass0", align_bytes=64)
+        deal(codes_pass0, picked_pass0, LINE_WORDS)
 
-        picked_scales = keep.tile([P, S], U8, name="picked_scales", tag="first")
+        picked_scales = keep.tile([P, S], U8, name="picked_scales", tag="picked_pass0")
         nc.vector.tensor_copy(picked_scales[:], scale_window[:].indirect(offsets[:]))
-        nc.vector.tensor_copy(
-            out=x_scale[:].rearrange("p d (c i) -> p c d i", i=16),
-            in_=picked_scales[:].rearrange("p (c i d) -> p c d i", i=16, d=D),
-        )
+        deal(x_scale, picked_scales, LINE_BYTES)
 
-        w1_bf = [
-            keep.tile([P, PACK, P, PACK], BF16, name="w1_bf0", tag="middle", align_bytes=64),
-            keep.tile([P, PACK, P, PACK], BF16, name="w1_bf1", tag="late", align_bytes=64),
-        ]
+        w1_bf = [keep.tile([P, PACK, P, PACK], BF16, name="w1_bf%d" % o, tag="w1_bf%d" % o, align_bytes=64) for o in range(PASSES)]
         w1_codes = [
-            keep.tile([P, H], U32, name="w1_codes0", tag="early", align_bytes=64),
+            keep.tile([P, H], U32, name="w1_codes0", tag="scale_window", align_bytes=64),
             keep.tile([P, H], U32, name="w1_codes1", align_bytes=64),
         ]
         w1_scale = [keep.tile([P, H], U8, name="w1_scale%d" % o, align_bytes=64) for o in range(PASSES)]
-        nc.scalar.copy(out=w1_bf[0][:].rearrange("p t m j -> p m t j"), in_=w1_raw0[:].rearrange("p j (m t) -> p m t j", t=PACK))
-        nc.vector.quantize_mx(out=w1_codes[0][:].bitcast(FP8X4), scales=w1_scale[0][:], in_=w1_bf[0][:].rearrange("p t m j -> p (t m j)"))
 
-        x_codes = {(0, b): codes_first[:, :, P * b : P * b + P] for b in range(BLOCKS)}
-
-        def pick_words(o, b):
-            if (o, b) == (1, 1):
-                picked = keep.tile([P, P * D], U32, name="picked_last", tag="late", align_bytes=64)
-            else:
-                picked = keep.tile([P, P * D], U32, name="picked_third", tag="middle", align_bytes=64)
-            nc.vector.tensor_copy(picked[:], word_window[o][:].indirect(offsets[:, 32 * b : 32 * b + 32]))
-            dealt = keep.tile([P, D, P], U32, name="x_codes%d_%d" % (o, b), align_bytes=64)
-            nc.vector.tensor_copy(
-                out=dealt[:].rearrange("p d (c i) -> p c d i", i=4),
-                in_=picked[:].rearrange("p (c i d) -> p c d i", i=4, d=D),
+        def quantize_w1(o):
+            nc.vector.quantize_mx(
+                out=w1_codes[o][:].bitcast(FP8X4), scales=w1_scale[o][:], in_=w1_bf[o][:].rearrange("p t m j -> p (t m j)")
             )
-            x_codes[o, b] = dealt
 
-        pick_words(1, 0)
+        nc.scalar.copy(out=w1_bf[0][:].rearrange("p t m j -> p m t j"), in_=w1_raw0[:].rearrange("p j (m t) -> p m t j", t=PACK))
+        quantize_w1(0)
+
+        x_codes = {(0, b): codes_pass0[:, :, P * b : P * b + P] for b in range(BLOCKS)}
+
+        def pick_pass1(b):
+            picked = keep.tile([P, P * D], U32, name="picked_pass1_%d" % b, tag="w1_bf%d" % b, align_bytes=64)
+            nc.vector.tensor_copy(picked[:], word_window[1][:].indirect(offsets[:, LIST_COLS * b : LIST_COLS * (b + 1)]))
+            dealt = keep.tile([P, D, P], U32, name="codes_pass1_%d" % b, align_bytes=64)
+            deal(dealt, picked, LINE_WORDS)
+            x_codes[1, b] = dealt
+
+        pick_pass1(0)
 
         for h in range(2):
-            ms = slice(HALF * h, HALF * h + HALF)
-            dst = w1_bf[1][:, :, ms, :].rearrange("p t m j -> p m t j")
+            dst = w1_bf[1][:, :, M_HALF * h : M_HALF * (h + 1), :].rearrange("p t m j -> p m t j")
             src = w1_raw1[h][:].rearrange("p j (m t) -> p m t j", t=PACK)
-            cut = 16 if h == 0 else 48
+            cut = VECTOR_M[h]
             nc.vector.tensor_copy(out=dst[:, 0:cut], in_=src[:, 0:cut])
-            nc.scalar.copy(out=dst[:, cut:HALF], in_=src[:, cut:HALF])
-        nc.vector.quantize_mx(out=w1_codes[1][:].bitcast(FP8X4), scales=w1_scale[1][:], in_=w1_bf[1][:].rearrange("p t m j -> p (t m j)"))
+            nc.scalar.copy(out=dst[:, cut:M_HALF], in_=src[:, cut:M_HALF])
+        quantize_w1(1)
 
-        pick_words(1, 1)
+        pick_pass1(1)
 
-        wo_bf = keep.tile([P, N, PACK], BF16, name="wo_bf", tag="raw1_1", align_bytes=64)
-        wo_dst = wo_bf[:].rearrange("p (c i) t -> p c t i", i=4)
-        wo_src = wo_raw[:].rearrange("p t (c i) -> p c t i", i=4)
-        nc.scalar.copy(out=wo_dst[:, 0:32], in_=wo_src[:, 0:32])
-        nc.vector.tensor_copy(out=wo_dst[:, 32:64], in_=wo_src[:, 32:64])
+        wo_bf = keep.tile([P, N, PACK], BF16, name="wo_bf", tag="w1_raw1_1", align_bytes=64)
+        wo_dst = wo_bf[:].rearrange("p (c i) j -> p c j i", i=4)
+        wo_src = wo_raw[:].rearrange("p j (c i) -> p c j i", i=4)
+        groups = N // 4
+        nc.scalar.copy(out=wo_dst[:, 0 : groups // 2], in_=wo_src[:, 0 : groups // 2])
+        nc.vector.tensor_copy(out=wo_dst[:, groups // 2 : groups], in_=wo_src[:, groups // 2 : groups])
         wo_codes = keep.tile([P, N], U32, name="wo_codes", align_bytes=64)
         wo_scale = keep.tile([P, N], U8, name="wo_scale", align_bytes=64)
-        nc.vector.quantize_mx(out=wo_codes[:].bitcast(FP8X4), scales=wo_scale[:], in_=wo_bf[:].rearrange("p c t -> p (c t)"))
+        nc.vector.quantize_mx(out=wo_codes[:].bitcast(FP8X4), scales=wo_scale[:], in_=wo_bf[:].rearrange("p n j -> p (n j)"))
 
-        den = {0: sums.tile([P, PACK, P], F32, name="den0", tag="den")}
-        num = {0: sums.tile([P, PACK, P], F32, name="num0", tag="num")}
-
-        tiles = [(b, d) for b in range(BLOCKS) for d in range(D)]
+        den = {0: sums.tile([P, PACK, P], F32, name="den0")}
+        num = {0: sums.tile([P, PACK, P], F32, name="num0")}
         ys, ths, hats = {}, {}, {}
 
         def product(u):
-            b, d = tiles[u]
-            y = ybanks.tile([P, H], F32, name="y", tag="y")
+            b, d = TILES[u]
+            y = ybanks.tile([P, H], F32, name="y", tag="bank")
             for o in range(PASSES):
                 nc.tensor.matmul_mx(
                     out=y[:],
                     lhsT=x_codes[o, b][:, d, :].bitcast(FP8X4),
-                    lhsT_scale=x_scale[4 * o :, d, P * b : P * b + P],
+                    lhsT_scale=x_scale[SCALE_ROWS * o :, d, P * b : P * b + P],
                     rhs=w1_codes[o][:].bitcast(FP8X4),
                     rhs_scale=w1_scale[o][:],
                     start=(o == 0),
@@ -156,94 +164,97 @@ def tile_picked_yhdrmg_mean_p_kernel(tc, x_words, x_scales, w1, logt, unit, wo, 
             ys[u] = y
 
         def squash(u):
-            y = ys[u]
-            if u == 6:
-                th = keep.tile([P, H], F32, name="th_last", tag="last")
+            if u == len(TILES) - 1:
+                th = keep.tile([P, H], F32, name="th_last", tag="th_last")
             else:
                 th = ring.tile([P, H], F32, name="th")
-            nc.scalar.activation(out=th[:], in_=y[:], func=ACT.Tanh, scale=0.5)
+            nc.scalar.activation(out=th[:], in_=ys[u][:], func=ACT.Tanh, scale=0.5)
             ths[u] = th
 
-        def weight(u):
-            th = ths[u]
-            sq = ring.tile([P, H], F32, name="sq")
-            if u in (3, 5, 7):
-                nc.vector.tensor_tensor(out=sq[:], in0=th[:], in1=th[:], op=ALU.mult)
-            else:
-                nc.scalar.activation(out=sq[:], in_=th[:], func=ACT.Square)
-            hat = ring.tile([P, H], F32, name="hat")
-            eng = nc.gpsimd if u in range(8) else nc.vector
-            eng.tensor_scalar(out=hat[:], in0=sq[:], scalar1=-0.25, scalar2=0.27, op0=ALU.mult, op1=ALU.add)
-            hats[u] = hat
-
-        def add_turned(u, src, acc):
-            d = tiles[u][1]
+        def add_turned(src, acc, first, last):
             for t in range(PACK):
                 nc.tensor.matmul(
                     out=acc[:, t, :],
                     lhsT=src[:, P * t : P * t + P],
                     rhs=ident[:],
                     is_transpose=True,
-                    start=(d == 0 and t == 0),
-                    stop=(d == D - 1 and t == PACK - 1),
+                    start=(first and t == 0),
+                    stop=(last and t == PACK - 1),
                 )
 
+        def weight(u):
+            b, d = TILES[u]
+            th = ths[u]
+            sq = ring.tile([P, H], F32, name="sq")
+            if u in VECTOR_SQUARES:
+                nc.vector.tensor_tensor(out=sq[:], in0=th[:], in1=th[:], op=ALU.mult)
+            else:
+                nc.scalar.activation(out=sq[:], in_=th[:], func=ACT.Square)
+            hat = ring.tile([P, H], F32, name="hat")
+            nc.gpsimd.tensor_scalar(out=hat[:], in0=sq[:], scalar1=-0.25, scalar2=0.27, op0=ALU.mult, op1=ALU.add)
+            hats[u] = hat
+            if b == 0:
+                add_turned(hat, den[b], d == 0, d == D - 1)
+            elif d % 2 == 1:
+                pair = ring.tile([P, H], F32, name="pair")
+                nc.vector.tensor_tensor(out=pair[:], in0=hats[u - 1][:], in1=hat[:], op=ALU.add)
+                if d == 1:
+                    den[b] = ybanks.tile([P, PACK, P], F32, name="den1", tag="bank")
+                add_turned(pair, den[b], d == 1, d == D - 1)
+
         def weighted(u):
-            b, d = tiles[u]
+            b, d = TILES[u]
             wl = ring.tile([P, H], F32, name="wl")
             nc.vector.scalar_tensor_tensor(
                 out=wl[:], in0=ys[u][:], scalar=logt_sb[:, b, d : d + 1], in1=hats[u][:], op0=ALU.subtract, op1=ALU.mult
             )
             if (b, d) == (1, 0):
-                den[1] = sums.tile([P, PACK, P], F32, name="den1")
-                num[1] = ybanks.tile([P, PACK, P], F32, name="num1", tag="y")
-            add_turned(u, hats[u], den[b])
-            add_turned(u, wl, num[b])
+                num[b] = ybanks.tile([P, PACK, P], F32, name="num1", tag="bank")
+            add_turned(wl, num[b], d == 0, d == D - 1)
 
         product(0)
         product(1)
-        for step in range(len(tiles) + 2):
-            if step + 2 < len(tiles):
+        for step in range(len(TILES) + 2):
+            if step + 2 < len(TILES):
                 product(step + 2)
-            if step < len(tiles):
+            if step < len(TILES):
                 squash(step)
-            if 1 <= step <= len(tiles):
+            if 1 <= step <= len(TILES):
                 weight(step - 1)
             if step >= 2:
                 weighted(step - 2)
 
-        inverses = []
-        for b in range(BLOCKS):
-            if b == 0:
-                rs = keep.tile([P, H], F32, name="rs0", tag="last")
-            else:
-                rs = keep.tile([P, H], F32, name="rs1")
+        root0 = keep.tile([P, H], F32, name="root0", tag="th_last")
+        root1 = keep.tile([P, H], F32, name="root1")
+        for b, root in enumerate((root0, root1)):
             nc.scalar.activation(
-                out=rs[:].rearrange("p (v t) -> p v t", t=PACK), in_=den[b][:].rearrange("p t v -> p v t"), func=ACT.Abs_reciprocal_sqrt
+                out=root[:].rearrange("p (v t) -> p v t", t=PACK), in_=den[b][:].rearrange("p t v -> p v t"), func=ACT.Abs_reciprocal_sqrt
             )
-            inverse = keep.tile([P, H], F32, name="inverse%d" % b)
-            nc.scalar.activation(out=inverse[:], in_=rs[:], func=ACT.Square)
-            inverses.append(inverse)
+        inverse1 = keep.tile([P, H], F32, name="inverse1")
+        nc.scalar.activation(out=inverse1[:], in_=root1[:], func=ACT.Square)
+        factors = ((root0, root0), (inverse1,))
 
         for b in range(BLOCKS):
-            inverse = inverses[b]
-            scaled = keep.tile([P, P, PACK], F32, name="scaled%d" % b)
+            value = keep.tile([P, H], F32, name="scaled%d" % b)
             nc.vector.tensor_tensor(
-                out=scaled[:],
+                out=value[:].rearrange("p (v t) -> p v t", t=PACK),
                 in0=num[b][:].rearrange("p t v -> p v t"),
                 in1=unit_sb[:].unsqueeze(1).to_broadcast([P, P, PACK]),
                 op=ALU.mult,
             )
-            zz = keep.tile([P, P, PACK], BF16, name="zz%d" % b, align_bytes=64)
-            nc.vector.tensor_tensor(
-                out=zz[:].rearrange("p v t -> p (v t)"), in0=scaled[:].rearrange("p v t -> p (v t)"), in1=inverse[:], op=ALU.mult
-            )
+            for factor in factors[b][:-1]:
+                partly = keep.tile([P, H], F32, name="partly%d" % b)
+                nc.vector.tensor_tensor(out=partly[:], in0=value[:], in1=factor[:], op=ALU.mult)
+                value = partly
+            zz = keep.tile([P, H], BF16, name="zz%d" % b, align_bytes=64)
+            nc.vector.tensor_tensor(out=zz[:], in0=value[:], in1=factors[b][-1][:], op=ALU.mult)
             zz_codes = keep.tile([P, P], U32, name="zz_codes%d" % b, align_bytes=64)
             zz_scale = keep.tile([P, P], U8, name="zz_scale%d" % b, align_bytes=64)
-            nc.vector.quantize_mx(out=zz_codes[:].bitcast(FP8X4), scales=zz_scale[:], in_=zz[:].rearrange("p v t -> p (v t)"))
-            acc = ybanks.tile([P, H], F32, name="acc", tag="y")
-            for m in range(N // P):
-                cols = slice(P * m, P * m + P)
+            nc.vector.quantize_mx(out=zz_codes[:].bitcast(FP8X4), scales=zz_scale[:], in_=zz[:])
+
+            acc = ybanks.tile([P, H], F32, name="acc", tag="bank")
+            for g in range(N // P):
+                cols = slice(P * g, P * g + P)
                 nc.tensor.matmul_mx(
                     out=acc[:, cols],
                     lhsT=wo_codes[:, cols].bitcast(FP8X4),
@@ -256,6 +267,6 @@ def tile_picked_yhdrmg_mean_p_kernel(tc, x_words, x_scales, w1, logt, unit, wo, 
             res = keep.tile([P, N], F32, name="res%d" % b)
             nc.scalar.copy(out=res[:], in_=acc[:, 0:N])
             nc.sync.dma_start(
-                out=out[:, P * b : P * b + P].rearrange("(m p) v -> p m v", p=P),
-                in_=res[:].rearrange("p (m v) -> p m v", v=P),
+                out=out[:, P * b : P * b + P].rearrange("(g p) v -> p g v", p=P),
+                in_=res[:].rearrange("p (g v) -> p g v", v=P),
             )

from contextlib import ExitStack

import concourse.mybir as mybir
from concourse.masks import make_identity

K, H, T, S, D, N = 1024, 512, 4096, 1024, 4, 256
V = S // D
FLOPS = 2 * K * H * S + 2 * H * N * V
BYTES = K * T + K * T // 32 + 4 * (K * H + S + H + H * N + N * V) + 2 * 128 * S // 16

F32 = mybir.dt.float32
BF16 = mybir.dt.bfloat16
I32 = mybir.dt.int32
U32 = mybir.dt.uint32
U16 = mybir.dt.uint16
U8 = mybir.dt.uint8
FP8X4 = mybir.dt.float8_e4m3fn_x4
ALU = mybir.AluOpType
ACT = mybir.ActivationFunctionType

P = 128
PACK = 4
K_PASS = P * PACK
PASSES = K // K_PASS
BLOCKS = V // P
TILES = [(b, d) for b in range(BLOCKS) for d in range(D)]
QUADRANT = 32
SCALE_ROWS = 4
LIST_COLS = P * D // 16
LINE_WORDS, LINE_BYTES = 4, 16
M_HALF = P // 2

Y_BANKS = 6
VECTOR_M = (16, 48)
VECTOR_SQUARES = (3, 5)


def tile_picked_yhdrmg_mean_p_kernel(tc, x_words, x_scales, w1, logt, unit, wo, offs, out):
    nc = tc.nc
    with ExitStack() as ctx:
        keep = ctx.enter_context(tc.tile_pool(name="keep", bufs=1))
        ring = ctx.enter_context(tc.tile_pool(name="ring", bufs=len(TILES)))
        ybanks = ctx.enter_context(tc.psum_pool(name="ybanks", bufs=Y_BANKS))
        sums = ctx.enter_context(tc.psum_pool(name="sums", bufs=1))

        offsets = keep.tile([P, S // 16], U16, name="offsets")
        nc.sync.dma_start(offsets[:], offs)

        scale_window = keep.tile([P, T], U8, name="scale_window", tag="scale_window", align_bytes=64)
        nc.vector.memset(scale_window[:].bitcast(I32), 0)
        word_window = [keep.tile([P, T], U32, name="word_window%d" % o) for o in range(PASSES)]

        def load_words(o, cols):
            src = x_words[o, :, cols, :].rearrange("p n t -> p (n t)").bitcast(I32)
            nc.sync.dma_start(out=word_window[o][:, cols].bitcast(I32), in_=src)

        for o in range(PASSES):
            load_words(0, slice(o * T // 2, (o + 1) * T // 2))
            for r in range(SCALE_ROWS):
                nc.sync.dma_start(
                    out=scale_window[SCALE_ROWS * o + r : P : QUADRANT, :].bitcast(I32),
                    in_=x_scales[o, r : K_PASS // 32 : SCALE_ROWS, :].bitcast(I32),
                )
        w1_raw0 = keep.tile([P, PACK, H], F32, name="w1_raw0")
        nc.sync.dma_start(out=w1_raw0[:], in_=w1[0:K_PASS, :].rearrange("(p j) c -> p j c", j=PACK))
        load_words(1, slice(0, T))

        w1_raw1 = []
        for h in range(2):
            raw = keep.tile([P, PACK, H // 2], F32, name="w1_raw1_%d" % h, tag="w1_raw1_%d" % h, align_bytes=64)
            cols = slice(h * H // 2, (h + 1) * H // 2)
            nc.sync.dma_start(out=raw[:], in_=w1[K_PASS:K, cols].rearrange("(p j) c -> p j c", j=PACK))
            w1_raw1.append(raw)

        wo_raw = keep.tile([P, PACK, N], F32, name="wo_raw")
        nc.sync.dma_start(out=wo_raw[:], in_=wo.rearrange("(p j) c -> p j c", j=PACK))
        logt_sb = keep.tile([P, BLOCKS, D], F32, name="logt_sb")
        nc.sync.dma_start(out=logt_sb[:], in_=logt[0].rearrange("(b p d) -> p b d", b=BLOCKS, d=D))
        unit_sb = keep.tile([P, PACK], F32, name="unit_sb")
        nc.sync.dma_start(out=unit_sb[:], in_=unit.rearrange("(p t) o -> p (t o)", t=PACK))

        ident = keep.tile([P, P], F32, name="ident")
        make_identity(nc, ident[:])

        def deal(dealt, picked, run):
            nc.vector.tensor_copy(
                out=dealt[:].rearrange("p d (c i) -> p c d i", i=run),
                in_=picked[:].rearrange("p (c i d) -> p c d i", i=run, d=D),
            )

        x_scale = keep.tile([P, D, V], U8, name="x_scale", align_bytes=64)
        picked_pass0 = keep.tile([P, S], U32, name="picked_pass0", tag="picked_pass0")
        nc.vector.tensor_copy(picked_pass0[:], word_window[0][:].indirect(offsets[:]))
        codes_pass0 = keep.tile([P, D, V], U32, name="codes_pass0", align_bytes=64)
        deal(codes_pass0, picked_pass0, LINE_WORDS)

        picked_scales = keep.tile([P, S], U8, name="picked_scales", tag="picked_pass0")
        nc.vector.tensor_copy(picked_scales[:], scale_window[:].indirect(offsets[:]))
        deal(x_scale, picked_scales, LINE_BYTES)

        w1_bf = [keep.tile([P, PACK, P, PACK], BF16, name="w1_bf%d" % o, tag="w1_bf%d" % o, align_bytes=64) for o in range(PASSES)]
        w1_codes = [
            keep.tile([P, H], U32, name="w1_codes0", tag="scale_window", align_bytes=64),
            keep.tile([P, H], U32, name="w1_codes1", align_bytes=64),
        ]
        w1_scale = [keep.tile([P, H], U8, name="w1_scale%d" % o, align_bytes=64) for o in range(PASSES)]

        def quantize_w1(o):
            nc.vector.quantize_mx(
                out=w1_codes[o][:].bitcast(FP8X4), scales=w1_scale[o][:], in_=w1_bf[o][:].rearrange("p t m j -> p (t m j)")
            )

        nc.scalar.copy(out=w1_bf[0][:].rearrange("p t m j -> p m t j"), in_=w1_raw0[:].rearrange("p j (m t) -> p m t j", t=PACK))
        quantize_w1(0)

        x_codes = {(0, b): codes_pass0[:, :, P * b : P * b + P] for b in range(BLOCKS)}

        def pick_pass1(b):
            picked = keep.tile([P, P * D], U32, name="picked_pass1_%d" % b, tag="w1_bf%d" % b, align_bytes=64)
            nc.vector.tensor_copy(picked[:], word_window[1][:].indirect(offsets[:, LIST_COLS * b : LIST_COLS * (b + 1)]))
            dealt = keep.tile([P, D, P], U32, name="codes_pass1_%d" % b, align_bytes=64)
            deal(dealt, picked, LINE_WORDS)
            x_codes[1, b] = dealt

        pick_pass1(0)

        for h in range(2):
            dst = w1_bf[1][:, :, M_HALF * h : M_HALF * (h + 1), :].rearrange("p t m j -> p m t j")
            src = w1_raw1[h][:].rearrange("p j (m t) -> p m t j", t=PACK)
            cut = VECTOR_M[h]
            nc.vector.tensor_copy(out=dst[:, 0:cut], in_=src[:, 0:cut])
            nc.scalar.copy(out=dst[:, cut:M_HALF], in_=src[:, cut:M_HALF])
        quantize_w1(1)

        pick_pass1(1)

        wo_bf = keep.tile([P, N, PACK], BF16, name="wo_bf", tag="w1_raw1_1", align_bytes=64)
        wo_dst = wo_bf[:].rearrange("p (c i) j -> p c j i", i=4)
        wo_src = wo_raw[:].rearrange("p j (c i) -> p c j i", i=4)
        groups = N // 4
        nc.scalar.copy(out=wo_dst[:, 0 : groups // 2], in_=wo_src[:, 0 : groups // 2])
        nc.vector.tensor_copy(out=wo_dst[:, groups // 2 : groups], in_=wo_src[:, groups // 2 : groups])
        wo_codes = keep.tile([P, N], U32, name="wo_codes", align_bytes=64)
        wo_scale = keep.tile([P, N], U8, name="wo_scale", align_bytes=64)
        nc.vector.quantize_mx(out=wo_codes[:].bitcast(FP8X4), scales=wo_scale[:], in_=wo_bf[:].rearrange("p n j -> p (n j)"))

        den = {0: sums.tile([P, PACK, P], F32, name="den0")}
        num = {0: sums.tile([P, PACK, P], F32, name="num0")}
        ys, ths, hats = {}, {}, {}

        def product(u):
            b, d = TILES[u]
            y = ybanks.tile([P, H], F32, name="y", tag="bank")
            for o in range(PASSES):
                nc.tensor.matmul_mx(
                    out=y[:],
                    lhsT=x_codes[o, b][:, d, :].bitcast(FP8X4),
                    lhsT_scale=x_scale[SCALE_ROWS * o :, d, P * b : P * b + P],
                    rhs=w1_codes[o][:].bitcast(FP8X4),
                    rhs_scale=w1_scale[o][:],
                    start=(o == 0),
                    stop=(o == PASSES - 1),
                )
            ys[u] = y

        def squash(u):
            if u == len(TILES) - 1:
                th = keep.tile([P, H], F32, name="th_last", tag="th_last")
            else:
                th = ring.tile([P, H], F32, name="th")
            nc.scalar.activation(out=th[:], in_=ys[u][:], func=ACT.Tanh, scale=0.5)
            ths[u] = th

        def add_turned(src, acc, first, last):
            for t in range(PACK):
                nc.tensor.matmul(
                    out=acc[:, t, :],
                    lhsT=src[:, P * t : P * t + P],
                    rhs=ident[:],
                    is_transpose=True,
                    start=(first and t == 0),
                    stop=(last and t == PACK - 1),
                )

        def weight(u):
            b, d = TILES[u]
            th = ths[u]
            sq = ring.tile([P, H], F32, name="sq")
            if u in VECTOR_SQUARES:
                nc.vector.tensor_tensor(out=sq[:], in0=th[:], in1=th[:], op=ALU.mult)
            else:
                nc.scalar.activation(out=sq[:], in_=th[:], func=ACT.Square)
            hat = ring.tile([P, H], F32, name="hat")
            nc.gpsimd.tensor_scalar(out=hat[:], in0=sq[:], scalar1=-0.25, scalar2=0.27, op0=ALU.mult, op1=ALU.add)
            hats[u] = hat
            if b == 0:
                add_turned(hat, den[b], d == 0, d == D - 1)
            elif d % 2 == 1:
                pair = ring.tile([P, H], F32, name="pair")
                nc.vector.tensor_tensor(out=pair[:], in0=hats[u - 1][:], in1=hat[:], op=ALU.add)
                if d == 1:
                    den[b] = ybanks.tile([P, PACK, P], F32, name="den1", tag="bank")
                add_turned(pair, den[b], d == 1, d == D - 1)

        def weighted(u):
            b, d = TILES[u]
            wl = ring.tile([P, H], F32, name="wl")
            nc.vector.scalar_tensor_tensor(
                out=wl[:], in0=ys[u][:], scalar=logt_sb[:, b, d : d + 1], in1=hats[u][:], op0=ALU.subtract, op1=ALU.mult
            )
            if (b, d) == (1, 0):
                num[b] = ybanks.tile([P, PACK, P], F32, name="num1", tag="bank")
            add_turned(wl, num[b], d == 0, d == D - 1)

        product(0)
        product(1)
        for step in range(len(TILES) + 2):
            if step + 2 < len(TILES):
                product(step + 2)
            if step < len(TILES):
                squash(step)
            if 1 <= step <= len(TILES):
                weight(step - 1)
            if step >= 2:
                weighted(step - 2)

        root0 = keep.tile([P, H], F32, name="root0", tag="th_last")
        root1 = keep.tile([P, H], F32, name="root1")
        for b, root in enumerate((root0, root1)):
            nc.scalar.activation(
                out=root[:].rearrange("p (v t) -> p v t", t=PACK), in_=den[b][:].rearrange("p t v -> p v t"), func=ACT.Abs_reciprocal_sqrt
            )
        inverse1 = keep.tile([P, H], F32, name="inverse1")
        nc.scalar.activation(out=inverse1[:], in_=root1[:], func=ACT.Square)
        factors = ((root0, root0), (inverse1,))

        for b in range(BLOCKS):
            value = keep.tile([P, H], F32, name="scaled%d" % b)
            nc.vector.tensor_tensor(
                out=value[:].rearrange("p (v t) -> p v t", t=PACK),
                in0=num[b][:].rearrange("p t v -> p v t"),
                in1=unit_sb[:].unsqueeze(1).to_broadcast([P, P, PACK]),
                op=ALU.mult,
            )
            for factor in factors[b][:-1]:
                partly = keep.tile([P, H], F32, name="partly%d" % b)
                nc.vector.tensor_tensor(out=partly[:], in0=value[:], in1=factor[:], op=ALU.mult)
                value = partly
            zz = keep.tile([P, H], BF16, name="zz%d" % b, align_bytes=64)
            nc.vector.tensor_tensor(out=zz[:], in0=value[:], in1=factors[b][-1][:], op=ALU.mult)
            zz_codes = keep.tile([P, P], U32, name="zz_codes%d" % b, align_bytes=64)
            zz_scale = keep.tile([P, P], U8, name="zz_scale%d" % b, align_bytes=64)
            nc.vector.quantize_mx(out=zz_codes[:].bitcast(FP8X4), scales=zz_scale[:], in_=zz[:])

            acc = ybanks.tile([P, H], F32, name="acc", tag="bank")
            for g in range(N // P):
                cols = slice(P * g, P * g + P)
                nc.tensor.matmul_mx(
                    out=acc[:, cols],
                    lhsT=wo_codes[:, cols].bitcast(FP8X4),
                    lhsT_scale=wo_scale[:, cols],
                    rhs=zz_codes[:].bitcast(FP8X4),
                    rhs_scale=zz_scale[:],
                    start=True,
                    stop=True,
                )
            res = keep.tile([P, N], F32, name="res%d" % b)
            nc.scalar.copy(out=res[:], in_=acc[:, 0:N])
            nc.sync.dma_start(
                out=out[:, P * b : P * b + P].rearrange("(g p) v -> p g v", p=P),
                in_=res[:].rearrange("p (g v) -> p g v", v=P),
            )
